import numpy as np
CORES = [50,52,122,124]
N = 4
T, CAP = 128, 112
def entries(a): return a.T.reshape(-1)
def pack(v, P): return np.ascontiguousarray(np.asarray(v, np.int32).reshape(-1, P).T)
def lists(rng, how):
    n = rng.integers(1, CAP + 1, N)
    if how == "none": n[rng.integers(N)] = 0; n[rng.integers(N)] = 0
    if how == "full": n[:] = CAP
    if how == "one": n[:] = 1
    if how == "void": n[:] = 0
    Kp = np.zeros((N, T), np.int32)
    for r in range(N): Kp[r, (np.arange(T - n[r], T) if how == "last" else rng.permutation(T)[:n[r]])] = 1
    return {"keep": np.stack([pack(Kp[r], 16) for r in range(N)])}
def setup_inputs(rng):
    return dict({"x": rng.standard_normal((N, 128, T), dtype=np.float32)}, **lists(rng, "uniform"))
def setup_inputs_full(rng):
    d = setup_inputs(rng); d.update(lists(rng, "full"))
    for k in ("x",): d[k] = (d[k].astype(np.float32) * 1048576.0).astype(d[k].dtype)
    return d
def setup_inputs_last(rng):
    d = setup_inputs(rng); d.update(lists(rng, "last"))
    for k in ("x",): d[k] = (d[k].astype(np.float32) * (1 / 1024.0)).astype(d[k].dtype)
    return d
def setup_inputs_none(rng):
    d = setup_inputs(rng); d.update(lists(rng, "none"))
    return d
def setup_inputs_one(rng):
    d = setup_inputs(rng); d.update(lists(rng, "one"))
    return d
def setup_inputs_void(rng):
    d = setup_inputs(rng); d.update(lists(rng, "void"))
    return d
def check_inputs(x):
    bad = []
    if x["keep"].min() < 0 or x["keep"].max() >= 2: bad.append("keep out of range")
    if max(int(a.sum()) for a in x["keep"]) > CAP: bad.append("a rank keeps more than CAP")
    return bad
def reference(x, keep):
    kept = np.concatenate([x[r][:, entries(keep[r]) == 1] for r in range(N)], axis=1)
    y = np.zeros((128, N * CAP), x.dtype); y[:, :kept.shape[1]] = kept
    return {"y": np.broadcast_to(y, (N, 128, N * CAP))}

@@ -1,0 +1,251 @@
+from concourse.bass import DstId, RemoteDMATransfer
+from concourse.mybir import AluOpType, ActivationFunctionType
+
+NCOL, OUTW, ZPAD = 128, 448, 4
+WINW = ZPAD + 4 * NCOL
+NSEM = 48
+
+SCRATCH = {
+    "win": ("sbuf", [128, WINW], "float32"),
+    "yb": ("sbuf", [128, OUTW], "float32"),
+    "F": ("sbuf", [128, 4], "int32"),
+    "kd": ("dram", [128, 1], "int32"),
+    "xd": ("dram", [128, NCOL], "float32"),
+    "Ji": ("sbuf", [128, 129], "int32"),
+    "L7": ("sbuf", [128, 129], "int32"),
+    "H3": ("sbuf", [128, 129], "int32"),
+    "L16": ("sbuf", [128, 129], "int32"),
+    "TQ": ("sbuf", [128, 129], "int32"),
+    "I15": ("sbuf", [128, 128], "int32"),
+    "tqf": ("sbuf", [128, 1], "float32"),
+    "tq4": ("sbuf", [128, 1], "float32"),
+    "Wc": ("sbuf", [128, 4], "int32"),
+    "WK": ("sbuf", [128, 4], "float32"),
+    "SL": ("sbuf", [128, 128], "float16"),
+    "one": ("sbuf", [128, 128], "float16"),
+    "I16": ("sbuf", [128, 128], "float16"),
+    "C16": ("sbuf", [128, 28], "float16"),
+    "Ff": ("sbuf", [128, 4], "float16"),
+    "G": ("sbuf", [128, 4], "float16"),
+    "a16": ("sbuf", [128, 4], "float32"),
+    "V": ("sbuf", [128, 4 * 128], "float16"),
+    "A": ("sbuf", [128, 4 * 28], "float16"),
+    "off": ("sbuf", [128, 28], "uint16"),
+    "pE": ("psum", [128, 512], "float32"),
+    "pO": ("psum", [128, 512], "float32"),
+}
+SEMAPHORES = ["ldk", "ldx", "ldkd", "ldd", "fl", "dat", "snt", "st"] + ["c%d" % k for k in range(NSEM)]
+
+
+def _bits(m):
+    return [b for b in range(16) if (m >> b) & 1]
+
+
+def _mk(bits):
+    m = 0
+    for b in bits:
+        m |= 1 << b
+    return m
+
+
+def _plan(T, topo):
+    ranks = list(T.cores)
+    used = set(ranks)
+    route = {}
+    for s in ranks:
+        for d in ranks:
+            if d == s:
+                continue
+            if topo.may_write(s, d):
+                route[(s, d)] = None
+                continue
+            cand = [c for c in range(topo.CHIPS * topo.CORES_PER_CHIP)
+                    if topo.chip(c) == topo.chip(s) and c not in used and topo.may_write(c, d)]
+            cand.sort(key=lambda c: (topo.die(c) != topo.die(s), c))
+            route[(s, d)] = cand[0]
+            used.add(cand[0])
+    return route
+
+
+def _calls(s, T, topo, route):
+    others = [d for d in T.cores if d != s]
+    near = [d for d in others if topo.chip(d) == topo.chip(s)]
+    far = [d for d in others if topo.chip(d) != topo.chip(s) and route[(s, d)] is None]
+    rel = [route[(s, d)] for d in others if route[(s, d)] is not None]
+    calls = []
+    if rel:
+        full = topo.mask(s, rel[0])
+        for c in rel + near:
+            full &= topo.mask(s, c)
+        b = _bits(full)
+        lo, hi = _mk(b[:len(b) // 2]), _mk(b[len(b) // 2:])
+        calls.append(("fl", [("dram", [(c, "dram") for c in rel], lo), ("dram", [(c, "sbuf") for c in near], hi)]))
+        calls.append(("dat", [("dram", [(c, "dram") for c in rel], full)]))
+        calls.append(("dat", [("dram", [(c, "sbuf") for c in near], full)]))
+    else:
+        moff = topo.mask(s, far[0])
+        for c in far:
+            moff &= topo.mask(s, c)
+        mon = topo.mask(s, near[0]) & ~moff
+        for kind in ("fl", "dat"):
+            calls.append((kind, [("sbuf", [(c, "sbuf") for c in far], moff), ("sbuf", [(c, "sbuf") for c in near], mon)]))
+    return calls
+
+
+def _expected(T, topo, route):
+    exp = {}
+    for s in T.cores:
+        for kind, trs in _calls(s, T, topo, route):
+            for _src, dsts, m in trs:
+                for c, _w in dsts:
+                    exp[(c, kind)] = exp.get((c, kind), 0) + len(_bits(m))
+    for (s, d), c in route.items():
+        if c is not None:
+            for kind in ("fl", "dat"):
+                exp[(d, kind)] = exp.get((d, kind), 0) + len(_bits(topo.mask(c, d)))
+    return exp
+
+
+def rank_program(g, core, T, topo):
+    route = _plan(T, topo)
+    exp = _expected(T, topo, route)
+    S = T.sem
+
+    def slot(r):
+        return T.win[:, ZPAD + NCOL * r:ZPAD + NCOL * (r + 1)]
+
+    for (s, d), c in route.items():
+        if c == core:
+            r = T.rank_of(s)
+            rid, pid, _se = topo.addr(d)
+            m = topo.mask(core, d)
+            g.wait_ge(S.fl, exp[(core, "fl")])
+            g.remote_dma(out_ap=T.F[:, r:r + 1], in_ap=T.kd[:, :], remote_sem=S.fl, local_sem=S.snt,
+                         pid=pid, routing_id=rid, dma_engine_mask=m)
+            g.wait_ge(S.dat, exp[(core, "dat")])
+            g.remote_dma(out_ap=slot(r), in_ap=T.xd[:, :], remote_sem=S.dat, local_sem=S.snt,
+                         pid=pid, routing_id=rid, dma_engine_mask=m)
+            g.wait_ge(S.snt, 2 * len(_bits(m)))
+            return
+    rank = T.rank_of(core)
+    if rank is None:
+        return
+
+    V, PE, SC, SY = g.vector, g.tensor, g.scalar, g.sync
+    Op = AluOpType
+    calls = _calls(core, T, topo, route)
+    by_relay = calls[0][1][0][0] == "dram"
+
+    if by_relay:
+        SC.dma_start(T.xd[:, :], T.x[:, :]).then_inc(S.ldd, 16)
+        SY.dma_start(T.kd[:, :], T.keep[:, :]).then_inc(S.ldkd, 16)
+        SY.dma_start(T.F[:, rank:rank + 1], T.keep[:, :]).then_inc(S.ldk, 16)
+        SY.dma_start(slot(rank), T.x[:, :]).then_inc(S.ldx, 16)
+    else:
+        SC.dma_start(slot(rank), T.x[:, :]).then_inc(S.ldx, 16)
+        SY.dma_start(T.F[:, rank:rank + 1], T.keep[:, :]).then_inc(S.ldk, 16)
+
+    n = [0]
+    seen = set()
+
+    def done(inst):
+        k = n[0]
+        n[0] += 1
+        inst.then_inc(S["c%d" % k], 1)
+        return k
+
+    def need(q, *ks):
+        for k in ks:
+            q.wait_ge(S["c%d" % k], 1)
+            seen.add(k)
+
+    i0 = done(g.iota(T.Ji[:, 0:128], [[1, 128]], 0, 0))
+    i1 = done(g.iota(T.Ji[:, 128:129], [[0, 1]], 0, 1))
+    zz = done(V.memset(T.win[:, 0:ZPAD], 0.0))
+    need(V, i0, i1)
+    k1 = done(V.tensor_scalar(T.L7[:, :], T.Ji[:, :], 7, None, Op.bitwise_and))
+    k2 = done(V.tensor_scalar(T.H3[:, :], T.Ji[:, :], 3, None, Op.logical_shift_right))
+    k8 = done(V.tensor_scalar(T.I15[:, :], T.Ji[:, 0:128], 15, None, Op.bitwise_and))
+    kone = done(V.tensor_scalar(T.one[:, :], T.Ji[:, 0:128], 0.0, None, Op.is_ge))
+    kc16 = done(V.tensor_scalar(T.C16[:, :], T.Ji[:, 0:28], 16.0, None, Op.mult))
+    kg0 = done(V.tensor_scalar(T.G[:, 0:1], T.Ji[:, 0:1], 0.0, -0.05859375, Op.mult, Op.add))
+    need(V, k1)
+    k3 = done(V.tensor_scalar(T.L16[:, :], T.L7[:, :], 16.0, None, Op.mult))
+    need(V, k8)
+    ki16 = done(V.tensor_scalar(T.I16[:, :], T.I15[:, :], -7.5, None, Op.add))
+    need(V, k2, k3)
+    k4 = done(V.tensor_tensor(T.TQ[:, :], T.L16[:, :], T.H3[:, :], Op.add))
+    need(V, k4)
+    k5 = done(V.tensor_copy(T.tqf[:, :], T.TQ[:, 128:129]))
+    k6 = done(V.tensor_scalar(T.tq4[:, :], T.TQ[:, 128:129], float(ZPAD), None, Op.add))
+    need(V, k5)
+    ksl = done(V.tensor_scalar(T.SL[:, :], T.TQ[:, 0:128], T.tqf[:, 0:1], None, Op.is_gt))
+    need(V, k6)
+    kwc = done(V.tensor_scalar(T.Wc[:, :], T.Ji[:, 0:4], float(NCOL), T.tq4[:, 0:1], Op.mult, Op.add))
+    need(V, kone, kc16, ki16, kwc)
+
+    sent = 0
+    first = {"fl": True, "dat": True}
+    for kind, trs in calls:
+        if first[kind]:
+            first[kind] = False
+            if kind == "fl":
+                g.wait_ge(S.ldkd if by_relay else S.ldk, 16)
+            else:
+                g.wait_ge(S.ldd if by_relay else S.ldx, 16)
+        tl = []
+        for src, dsts, m in trs:
+            if kind == "fl":
+                sap = T.kd[:, :] if src == "dram" else T.F[:, rank:rank + 1]
+                daps = [T.kd[:, :] if w == "dram" else T.F[:, rank:rank + 1] for _c, w in dsts]
+            else:
+                sap = T.xd[:, :] if src == "dram" else slot(rank)
+                daps = [T.xd[:, :] if w == "dram" else slot(rank) for _c, w in dsts]
+            ids = [DstId(rid=topo.addr(c)[0], pnc=topo.addr(c)[1]) for c, _w in dsts]
+            tl.append(RemoteDMATransfer(dst_ids=ids, dma_engine_mask=m, remote_sem=S[kind], srcs=[sap], dsts=daps))
+            sent += len(_bits(m))
+        g.remote_dma_fused(tl, local_sem=S.snt)
+
+    V.wait_ge(S.ldk, 16)
+    V.wait_ge(S.fl, exp[(core, "fl")])
+    kf = done(V.tensor_copy(T.Ff[:, :], T.F[:, :]))
+    need(V, kf)
+    kg = done(V.tensor_tensor_scan(T.G[:, 1:4], T.one[:, 0:3], T.Ff[:, 0:3], -0.05859375, Op.mult, Op.add))
+    kwk = done(V.tensor_tensor(T.WK[:, :], T.F[:, :], T.Wc[:, :], Op.mult))
+    need(PE, ksl, kone, kf)
+    PE.matmul(T.pE[:, 0:4], T.SL[:, :], T.Ff[:, :], True, False)
+    need(PE, kg0, kg)
+    ke = done(PE.matmul(T.pE[:, 0:4], T.one[:, :], T.G[:, :], False, True))
+    need(V, ke)
+    big = 201326592.0
+    ka = done(V.tensor_scalar(T.a16[:, :], T.pE[:, 0:4], big, big, Op.add, Op.subtract))
+    need(V, ka, kwk)
+    ko = None
+    for r in range(4):
+        kv = done(V.tensor_scalar(T.V[:, 128 * r:128 * (r + 1)], T.I16[:, :], T.a16[:, r:r + 1], T.pE[:, r:r + 1],
+                                  Op.add, Op.is_equal))
+        kA = done(V.tensor_scalar(T.A[:, 28 * r:28 * (r + 1)], T.C16[:, :], T.a16[:, r:r + 1], T.WK[:, r:r + 1],
+                                  Op.is_equal, Op.mult))
+        need(PE, kv, kA)
+        mm = PE.matmul(T.pO[:, 0:28], T.V[:, 128 * r:128 * (r + 1)], T.A[:, 28 * r:28 * (r + 1)], r == 0, r == 3)
+        if r == 3:
+            ko = done(mm)
+    need(V, ko)
+    kl = done(V.tensor_copy(T.off[:, :], T.pO[:, 0:28]))
+
+    need(V, kl, zz)
+    V.wait_ge(S.ldx, 16)
+    V.wait_ge(S.dat, exp[(core, "dat")])
+    g1 = done(V.tensor_copy(T.yb[:, 0:224], T.win[:, 0:WINW].indirect(T.off[:, 0:14])))
+    need(SC, kl, zz)
+    SC.wait_ge(S.ldx, 16)
+    SC.wait_ge(S.dat, exp[(core, "dat")])
+    g2 = done(SC.activation(T.yb[:, 224:448], T.win[:, 0:WINW].indirect(T.off[:, 14:28]), ActivationFunctionType.Copy))
+    need(SY, g1, g2)
+    SY.dma_start(T.y[:, :], T.yb[:, :]).then_inc(S.st, 16)
+    SY.wait_ge(S.st, 16)
+
+    g.wait_ge(S.snt, sent)
+    for k in range(n[0]):
+        if k not in seen:
+            g.wait_ge(S["c%d" % k], 1)

@@ -18,13 +18,12 @@ SCRATCH = {
     "TQ": ("sbuf", [128, 129], "int32"),
     "I15": ("sbuf", [128, 128], "int32"),
     "tqf": ("sbuf", [128, 1], "float32"),
-    "tq4": ("sbuf", [128, 1], "float32"),
+    "TB": ("sbuf", [128, 32], "int32"),
     "Wc": ("sbuf", [128, 4], "int32"),
     "WK": ("sbuf", [128, 4], "float32"),
     "SL": ("sbuf", [128, 128], "float16"),
     "one": ("sbuf", [128, 128], "float16"),
     "I16": ("sbuf", [128, 128], "float16"),
-    "C16": ("sbuf", [128, 28], "float16"),
     "Ff": ("sbuf", [128, 4], "float16"),
     "G": ("sbuf", [128, 4], "float16"),
     "a16": ("sbuf", [128, 4], "float32"),
@@ -34,7 +33,7 @@ SCRATCH = {
     "pE": ("psum", [128, 512], "float32"),
     "pO": ("psum", [128, 512], "float32"),
 }
-SEMAPHORES = ["ldk", "ldx", "ldkd", "ldd", "fl", "dat", "snt", "st"] + ["c%d" % k for k in range(NSEM)]
+SEMAPHORES = ["ldk", "ldx", "ldkd", "ldd", "fl", "dat", "snt", "st", "tb", "ti"] + ["c%d" % k for k in range(NSEM)]
 
 
 def _bits(m):
@@ -106,9 +105,24 @@ def _expected(T, topo, route):
     return exp
 
 
+def _feeder(T, route):
+    f = {d: None for d in T.cores}
+    for (_s, d), c in route.items():
+        if c is not None and f[d] is None:
+            f[d] = c
+    return f
+
+
+def _piece(core, T, topo):
+    grp = [c for c in T.cores if topo.chip(c) == topo.chip(core)]
+    k, n = grp.index(core), len(grp)
+    return [c for c in grp if c != core], 4 * round(7 * k / n), 4 * round(7 * (k + 1) / n)
+
+
 def rank_program(g, core, T, topo):
     route = _plan(T, topo)
     exp = _expected(T, topo, route)
+    feeder = _feeder(T, route)
     S = T.sem
 
     def slot(r):
@@ -119,13 +133,20 @@ def rank_program(g, core, T, topo):
             r = T.rank_of(s)
             rid, pid, _se = topo.addr(d)
             m = topo.mask(core, d)
+            ncall = 2
+            if feeder[d] == core:
+                g.iota(T.TB[:, 28:32], [[NCOL, 4]], ZPAD, 0).then_inc(S.ti, 1)
+                g.wait_ge(S.ti, 1)
+                g.remote_dma(out_ap=T.TB[:, 28:32], in_ap=T.TB[:, 28:32], remote_sem=S.tb, local_sem=S.snt,
+                             pid=pid, routing_id=rid, dma_engine_mask=m)
+                ncall = 3
             g.wait_ge(S.fl, exp[(core, "fl")])
             g.remote_dma(out_ap=T.F[:, r:r + 1], in_ap=T.kd[:, :], remote_sem=S.fl, local_sem=S.snt,
                          pid=pid, routing_id=rid, dma_engine_mask=m)
             g.wait_ge(S.dat, exp[(core, "dat")])
             g.remote_dma(out_ap=slot(r), in_ap=T.xd[:, :], remote_sem=S.dat, local_sem=S.snt,
                          pid=pid, routing_id=rid, dma_engine_mask=m)
-            g.wait_ge(S.snt, 2 * len(_bits(m)))
+            g.wait_ge(S.snt, ncall * len(_bits(m)))
             return
     rank = T.rank_of(core)
     if rank is None:
@@ -159,6 +180,25 @@ def rank_program(g, core, T, topo):
             q.wait_ge(S["c%d" % k], 1)
             seen.add(k)
 
+    mates_, ta, tz = _piece(core, T, topo)
+    g.iota(T.TB[:, ta:tz], [[16, tz - ta]], 16 * ta, 0).then_inc(S.ti, 1)
+    nti, ntb, sent = 1, 0, 0
+    if feeder[core] is None:
+        g.iota(T.TB[:, 28:32], [[NCOL, 4]], ZPAD, 0).then_inc(S.ti, 1)
+        nti = 2
+    else:
+        ntb += len(_bits(topo.mask(feeder[core], core)))
+    g.wait_ge(S.ti, nti)
+    if mates_:
+        mt = topo.mask(core, mates_[0])
+        for c in mates_:
+            mt &= topo.mask(core, c)
+            ntb += len(_bits(topo.mask(c, core)))
+        g.remote_dma_fused([RemoteDMATransfer(dst_ids=[DstId(rid=topo.addr(c)[0], pnc=topo.addr(c)[1]) for c in mates_],
+                                              dma_engine_mask=mt, remote_sem=S.tb, srcs=[T.TB[:, ta:tz]],
+                                              dsts=[T.TB[:, ta:tz] for _c in mates_])], local_sem=S.snt)
+        sent += len(_bits(mt))
+
     i0 = done(g.iota(T.Ji[:, 0:128], [[1, 128]], 0, 0))
     i1 = done(g.iota(T.Ji[:, 128:129], [[0, 1]], 0, 1))
     zz = done(V.memset(T.win[:, 0:ZPAD], 0.0))
@@ -167,7 +207,6 @@ def rank_program(g, core, T, topo):
     k2 = done(V.tensor_scalar(T.H3[:, :], T.Ji[:, :], 3, None, Op.logical_shift_right))
     k8 = done(V.tensor_scalar(T.I15[:, :], T.Ji[:, 0:128], 15, None, Op.bitwise_and))
     kone = done(V.tensor_scalar(T.one[:, :], T.Ji[:, 0:128], 0.0, None, Op.is_ge))
-    kc16 = done(V.tensor_scalar(T.C16[:, :], T.Ji[:, 0:28], 16.0, None, Op.mult))
     kg0 = done(V.tensor_scalar(T.G[:, 0:1], T.Ji[:, 0:1], 0.0, -0.05859375, Op.mult, Op.add))
     need(V, k1)
     k3 = done(V.tensor_scalar(T.L16[:, :], T.L7[:, :], 16.0, None, Op.mult))
@@ -177,14 +216,14 @@ def rank_program(g, core, T, topo):
     k4 = done(V.tensor_tensor(T.TQ[:, :], T.L16[:, :], T.H3[:, :], Op.add))
     need(V, k4)
     k5 = done(V.tensor_copy(T.tqf[:, :], T.TQ[:, 128:129]))
-    k6 = done(V.tensor_scalar(T.tq4[:, :], T.TQ[:, 128:129], float(ZPAD), None, Op.add))
     need(V, k5)
     ksl = done(V.tensor_scalar(T.SL[:, :], T.TQ[:, 0:128], T.tqf[:, 0:1], None, Op.is_gt))
-    need(V, k6)
-    kwc = done(V.tensor_scalar(T.Wc[:, :], T.Ji[:, 0:4], float(NCOL), T.tq4[:, 0:1], Op.mult, Op.add))
-    need(V, kone, kc16, ki16, kwc)
+    V.wait_ge(S.ti, nti)
+    if ntb:
+        V.wait_ge(S.tb, ntb)
+    kwc = done(V.tensor_scalar(T.Wc[:, :], T.TB[:, 28:32], T.tqf[:, 0:1], None, Op.add))
+    need(V, kone, ki16, kwc)
 
-    sent = 0
     first = {"fl": True, "dat": True}
     for kind, trs in calls:
         if first[kind]:
@@ -224,7 +263,7 @@ def rank_program(g, core, T, topo):
     for r in range(4):
         kv = done(V.tensor_scalar(T.V[:, 128 * r:128 * (r + 1)], T.I16[:, :], T.a16[:, r:r + 1], T.pE[:, r:r + 1],
                                   Op.add, Op.is_equal))
-        kA = done(V.tensor_scalar(T.A[:, 28 * r:28 * (r + 1)], T.C16[:, :], T.a16[:, r:r + 1], T.WK[:, r:r + 1],
+        kA = done(V.tensor_scalar(T.A[:, 28 * r:28 * (r + 1)], T.TB[:, 0:28], T.a16[:, r:r + 1], T.WK[:, r:r + 1],
                                   Op.is_equal, Op.mult))
         need(PE, kv, kA)
         mm = PE.matmul(T.pO[:, 0:28], T.V[:, 128 * r:128 * (r + 1)], T.A[:, 28 * r:28 * (r + 1)], r == 0, r == 3)

@@ -11,6 +11,8 @@ SCRATCH = {
     "F": ("sbuf", [128, 4], "int32"),
     "kd": ("dram", [128, 1], "int32"),
     "xd": ("dram", [128, NCOL], "float32"),
+    "o32": ("sbuf", [128, 128], "float32"),
+    "Jf": ("sbuf", [128, 128], "float32"),
     "Ji": ("sbuf", [128, 129], "int32"),
     "L7": ("sbuf", [128, 129], "int32"),
     "H3": ("sbuf", [128, 129], "int32"),
@@ -18,12 +20,13 @@ SCRATCH = {
     "TQ": ("sbuf", [128, 129], "int32"),
     "I15": ("sbuf", [128, 128], "int32"),
     "tqf": ("sbuf", [128, 1], "float32"),
-    "TB": ("sbuf", [128, 32], "int32"),
+    "TB": ("sbuf", [128, 16], "int32"),
     "Wc": ("sbuf", [128, 4], "int32"),
     "WK": ("sbuf", [128, 4], "float32"),
     "SL": ("sbuf", [128, 128], "float16"),
     "one": ("sbuf", [128, 128], "float16"),
     "I16": ("sbuf", [128, 128], "float16"),
+    "C16": ("sbuf", [128, 28], "float16"),
     "Ff": ("sbuf", [128, 4], "float16"),
     "G": ("sbuf", [128, 4], "float16"),
     "a16": ("sbuf", [128, 4], "float32"),
@@ -66,26 +69,44 @@ def _plan(T, topo):
     return route
 
 
-def _calls(s, T, topo, route):
+def _sets(s, T, topo, route):
     others = [d for d in T.cores if d != s]
     near = [d for d in others if topo.chip(d) == topo.chip(s)]
     far = [d for d in others if topo.chip(d) != topo.chip(s) and route[(s, d)] is None]
     rel = [route[(s, d)] for d in others if route[(s, d)] is not None]
+    return near, far, rel
+
+
+def _masks(s, T, topo, route):
+    near, far, rel = _sets(s, T, topo, route)
+    full = topo.mask(s, near[0])
+    for c in near + rel:
+        full &= topo.mask(s, c)
+    moff = full
+    for c in far:
+        moff &= topo.mask(s, c)
+    return moff, full & ~moff, full
+
+
+def _early(s, T, topo, route):
+    near, far, _rel = _sets(s, T, topo, route)
+    moff, mon, full = _masks(s, T, topo, route)
+    if far:
+        return [(far, moff), (near, mon)]
+    return [(near, full)]
+
+
+def _calls(s, T, topo, route):
+    near, far, rel = _sets(s, T, topo, route)
+    moff, mon, full = _masks(s, T, topo, route)
     calls = []
     if rel:
-        full = topo.mask(s, rel[0])
-        for c in rel + near:
-            full &= topo.mask(s, c)
         b = _bits(full)
         lo, hi = _mk(b[:len(b) // 2]), _mk(b[len(b) // 2:])
         calls.append(("fl", [("dram", [(c, "dram") for c in rel], lo), ("dram", [(c, "sbuf") for c in near], hi)]))
         calls.append(("dat", [("dram", [(c, "dram") for c in rel], full)]))
         calls.append(("dat", [("dram", [(c, "sbuf") for c in near], full)]))
     else:
-        moff = topo.mask(s, far[0])
-        for c in far:
-            moff &= topo.mask(s, c)
-        mon = topo.mask(s, near[0]) & ~moff
         for kind in ("fl", "dat"):
             calls.append((kind, [("sbuf", [(c, "sbuf") for c in far], moff), ("sbuf", [(c, "sbuf") for c in near], mon)]))
     return calls
@@ -93,66 +114,58 @@ def _calls(s, T, topo, route):
 
 def _expected(T, topo, route):
     exp = {}
+
+    def add(c, kind, m):
+        exp[(c, kind)] = exp.get((c, kind), 0) + len(_bits(m))
+
     for s in T.cores:
+        for dsts, m in _early(s, T, topo, route):
+            for c in dsts:
+                add(c, "tb", m)
         for kind, trs in _calls(s, T, topo, route):
             for _src, dsts, m in trs:
                 for c, _w in dsts:
-                    exp[(c, kind)] = exp.get((c, kind), 0) + len(_bits(m))
-    for (s, d), c in route.items():
-        if c is not None:
-            for kind in ("fl", "dat"):
-                exp[(d, kind)] = exp.get((d, kind), 0) + len(_bits(topo.mask(c, d)))
-    return exp
-
-
-def _feeder(T, route):
-    f = {d: None for d in T.cores}
+                    add(c, kind, m)
     for (_s, d), c in route.items():
-        if c is not None and f[d] is None:
-            f[d] = c
-    return f
-
-
-def _piece(core, T, topo):
-    grp = [c for c in T.cores if topo.chip(c) == topo.chip(core)]
-    k, n = grp.index(core), len(grp)
-    return [c for c in grp if c != core], 4 * round(7 * k / n), 4 * round(7 * (k + 1) / n)
+        if c is not None:
+            for kind in ("tb", "fl", "dat"):
+                add(d, kind, topo.mask(c, d))
+    return exp
 
 
 def rank_program(g, core, T, topo):
     route = _plan(T, topo)
     exp = _expected(T, topo, route)
-    feeder = _feeder(T, route)
     S = T.sem
+    V, PE, SC, SY = g.vector, g.tensor, g.scalar, g.sync
 
     def slot(r):
         return T.win[:, ZPAD + NCOL * r:ZPAD + NCOL * (r + 1)]
+
+    def entry(r):
+        return T.TB[:, 4 * r:4 * r + 1]
 
     for (s, d), c in route.items():
         if c == core:
             r = T.rank_of(s)
             rid, pid, _se = topo.addr(d)
             m = topo.mask(core, d)
-            ncall = 2
-            if feeder[d] == core:
-                g.iota(T.TB[:, 28:32], [[NCOL, 4]], ZPAD, 0).then_inc(S.ti, 1)
-                g.wait_ge(S.ti, 1)
-                g.remote_dma(out_ap=T.TB[:, 28:32], in_ap=T.TB[:, 28:32], remote_sem=S.tb, local_sem=S.snt,
-                             pid=pid, routing_id=rid, dma_engine_mask=m)
-                ncall = 3
+            V.memset(entry(r), ZPAD + NCOL * r).then_inc(S.ti, 1)
+            g.wait_ge(S.ti, 1)
+            g.remote_dma(out_ap=entry(r), in_ap=entry(r), remote_sem=S.tb, local_sem=S.snt,
+                         pid=pid, routing_id=rid, dma_engine_mask=m)
             g.wait_ge(S.fl, exp[(core, "fl")])
             g.remote_dma(out_ap=T.F[:, r:r + 1], in_ap=T.kd[:, :], remote_sem=S.fl, local_sem=S.snt,
                          pid=pid, routing_id=rid, dma_engine_mask=m)
             g.wait_ge(S.dat, exp[(core, "dat")])
             g.remote_dma(out_ap=slot(r), in_ap=T.xd[:, :], remote_sem=S.dat, local_sem=S.snt,
                          pid=pid, routing_id=rid, dma_engine_mask=m)
-            g.wait_ge(S.snt, ncall * len(_bits(m)))
+            g.wait_ge(S.snt, 3 * len(_bits(m)))
             return
     rank = T.rank_of(core)
     if rank is None:
         return
 
-    V, PE, SC, SY = g.vector, g.tensor, g.scalar, g.sync
     Op = AluOpType
     calls = _calls(core, T, topo, route)
     by_relay = calls[0][1][0][0] == "dram"
@@ -180,33 +193,32 @@ def rank_program(g, core, T, topo):
             q.wait_ge(S["c%d" % k], 1)
             seen.add(k)
 
-    mates_, ta, tz = _piece(core, T, topo)
-    g.iota(T.TB[:, ta:tz], [[16, tz - ta]], 16 * ta, 0).then_inc(S.ti, 1)
-    nti, ntb, sent = 1, 0, 0
-    if feeder[core] is None:
-        g.iota(T.TB[:, 28:32], [[NCOL, 4]], ZPAD, 0).then_inc(S.ti, 1)
-        nti = 2
-    else:
-        ntb += len(_bits(topo.mask(feeder[core], core)))
-    g.wait_ge(S.ti, nti)
-    if mates_:
-        mt = topo.mask(core, mates_[0])
-        for c in mates_:
-            mt &= topo.mask(core, c)
-            ntb += len(_bits(topo.mask(c, core)))
-        g.remote_dma_fused([RemoteDMATransfer(dst_ids=[DstId(rid=topo.addr(c)[0], pnc=topo.addr(c)[1]) for c in mates_],
-                                              dma_engine_mask=mt, remote_sem=S.tb, srcs=[T.TB[:, ta:tz]],
-                                              dsts=[T.TB[:, ta:tz] for _c in mates_])], local_sem=S.snt)
-        sent += len(_bits(mt))
+    def ids(cs):
+        return [DstId(rid=topo.addr(c)[0], pnc=topo.addr(c)[1]) for c in cs]
 
-    i0 = done(g.iota(T.Ji[:, 0:128], [[1, 128]], 0, 0))
+    V.memset(entry(rank), ZPAD + NCOL * rank).then_inc(S.ti, 1)
+    g.wait_ge(S.ti, 1)
+    sent = 0
+    tl = []
+    for dsts, m in _early(core, T, topo, route):
+        tl.append(RemoteDMATransfer(dst_ids=ids(dsts), dma_engine_mask=m, remote_sem=S.tb, srcs=[entry(rank)],
+                                    dsts=[entry(rank) for _c in dsts]))
+        sent += len(_bits(m))
+    g.remote_dma_fused(tl, local_sem=S.snt)
+
     i1 = done(g.iota(T.Ji[:, 128:129], [[0, 1]], 0, 1))
+    ko32 = done(V.memset(T.o32[:, :], 1.0))
     zz = done(V.memset(T.win[:, 0:ZPAD], 0.0))
+    need(V, ko32)
+    kjf = done(V.tensor_tensor_scan(T.Jf[:, :], T.o32[:, :], T.o32[:, :], -1.0, Op.mult, Op.add))
+    need(V, kjf)
+    i0 = done(V.tensor_copy(T.Ji[:, 0:128], T.Jf[:, :]))
     need(V, i0, i1)
     k1 = done(V.tensor_scalar(T.L7[:, :], T.Ji[:, :], 7, None, Op.bitwise_and))
     k2 = done(V.tensor_scalar(T.H3[:, :], T.Ji[:, :], 3, None, Op.logical_shift_right))
     k8 = done(V.tensor_scalar(T.I15[:, :], T.Ji[:, 0:128], 15, None, Op.bitwise_and))
     kone = done(V.tensor_scalar(T.one[:, :], T.Ji[:, 0:128], 0.0, None, Op.is_ge))
+    kc16 = done(V.tensor_scalar(T.C16[:, :], T.Ji[:, 0:28], 16.0, None, Op.mult))
     kg0 = done(V.tensor_scalar(T.G[:, 0:1], T.Ji[:, 0:1], 0.0, -0.05859375, Op.mult, Op.add))
     need(V, k1)
     k3 = done(V.tensor_scalar(T.L16[:, :], T.L7[:, :], 16.0, None, Op.mult))
@@ -218,11 +230,10 @@ def rank_program(g, core, T, topo):
     k5 = done(V.tensor_copy(T.tqf[:, :], T.TQ[:, 128:129]))
     need(V, k5)
     ksl = done(V.tensor_scalar(T.SL[:, :], T.TQ[:, 0:128], T.tqf[:, 0:1], None, Op.is_gt))
-    V.wait_ge(S.ti, nti)
-    if ntb:
-        V.wait_ge(S.tb, ntb)
-    kwc = done(V.tensor_scalar(T.Wc[:, :], T.TB[:, 28:32], T.tqf[:, 0:1], None, Op.add))
-    need(V, kone, ki16, kwc)
+    V.wait_ge(S.ti, 1)
+    V.wait_ge(S.tb, exp[(core, "tb")])
+    kwc = [done(V.tensor_scalar(T.Wc[:, r:r + 1], entry(r), T.tqf[:, 0:1], None, Op.add)) for r in range(4)]
+    need(V, kone, kc16, ki16, *kwc)
 
     first = {"fl": True, "dat": True}
     for kind, trs in calls:
@@ -240,8 +251,8 @@ def rank_program(g, core, T, topo):
             else:
                 sap = T.xd[:, :] if src == "dram" else slot(rank)
                 daps = [T.xd[:, :] if w == "dram" else slot(rank) for _c, w in dsts]
-            ids = [DstId(rid=topo.addr(c)[0], pnc=topo.addr(c)[1]) for c, _w in dsts]
-            tl.append(RemoteDMATransfer(dst_ids=ids, dma_engine_mask=m, remote_sem=S[kind], srcs=[sap], dsts=daps))
+            tl.append(RemoteDMATransfer(dst_ids=ids([c for c, _w in dsts]), dma_engine_mask=m, remote_sem=S[kind],
+                                        srcs=[sap], dsts=daps))
             sent += len(_bits(m))
         g.remote_dma_fused(tl, local_sem=S.snt)
 
@@ -263,7 +274,7 @@ def rank_program(g, core, T, topo):
     for r in range(4):
         kv = done(V.tensor_scalar(T.V[:, 128 * r:128 * (r + 1)], T.I16[:, :], T.a16[:, r:r + 1], T.pE[:, r:r + 1],
                                   Op.add, Op.is_equal))
-        kA = done(V.tensor_scalar(T.A[:, 28 * r:28 * (r + 1)], T.TB[:, 0:28], T.a16[:, r:r + 1], T.WK[:, r:r + 1],
+        kA = done(V.tensor_scalar(T.A[:, 28 * r:28 * (r + 1)], T.C16[:, :], T.a16[:, r:r + 1], T.WK[:, r:r + 1],
                                   Op.is_equal, Op.mult))
         need(PE, kv, kA)
         mm = PE.matmul(T.pO[:, 0:28], T.V[:, 128 * r:128 * (r + 1)], T.A[:, 28 * r:28 * (r + 1)], r == 0, r == 3)

@@ -3,7 +3,7 @@ from concourse.mybir import AluOpType, ActivationFunctionType
 
 NCOL, OUTW, ZPAD = 128, 448, 4
 WINW = ZPAD + 4 * NCOL
-NSEM = 48
+NSEM = 60
 
 SCRATCH = {
     "win": ("sbuf", [128, WINW], "float32"),
@@ -13,6 +13,7 @@ SCRATCH = {
     "xd": ("dram", [128, NCOL], "float32"),
     "o32": ("sbuf", [128, 128], "float32"),
     "Jf": ("sbuf", [128, 128], "float32"),
+    "JT": ("sbuf", [128, 128], "float32"),
     "Ji": ("sbuf", [128, 129], "int32"),
     "L7": ("sbuf", [128, 129], "int32"),
     "H3": ("sbuf", [128, 129], "int32"),
@@ -90,10 +91,11 @@ def _masks(s, T, topo, route):
 
 def _early(s, T, topo, route):
     near, far, _rel = _sets(s, T, topo, route)
-    moff, mon, full = _masks(s, T, topo, route)
+    moff, _mon, full = _masks(s, T, topo, route)
     if far:
-        return [(far, moff), (near, mon)]
-    return [(near, full)]
+        return [(near, moff)]
+    b = _bits(full)
+    return [(near, _mk(b[len(b) // 2:]))]
 
 
 def _calls(s, T, topo, route):
@@ -102,13 +104,15 @@ def _calls(s, T, topo, route):
     calls = []
     if rel:
         b = _bits(full)
-        lo, hi = _mk(b[:len(b) // 2]), _mk(b[len(b) // 2:])
-        calls.append(("fl", [("dram", [(c, "dram") for c in rel], lo), ("dram", [(c, "sbuf") for c in near], hi)]))
+        one, hi = _mk(b[:1]), _mk(b[len(b) // 2:])
+        calls.append(("fl", [("dram", [(c, "dram") for c in rel], one), ("dram", [(c, "sbuf") for c in near], hi)]))
         calls.append(("dat", [("dram", [(c, "dram") for c in rel], full)]))
         calls.append(("dat", [("dram", [(c, "sbuf") for c in near], full)]))
     else:
-        for kind in ("fl", "dat"):
-            calls.append((kind, [("sbuf", [(c, "sbuf") for c in far], moff), ("sbuf", [(c, "sbuf") for c in near], mon)]))
+        b = _bits(mon)
+        calls.append(("fl", [("dram", [(c, "sbuf") for c in far], moff),
+                             ("dram", [(c, "sbuf") for c in near], _mk(b[:len(b) // 2]))]))
+        calls.append(("dat", [("sbuf", [(c, "sbuf") for c in far], moff), ("sbuf", [(c, "sbuf") for c in near], mon)]))
     return calls
 
 
@@ -168,11 +172,11 @@ def rank_program(g, core, T, topo):
 
     Op = AluOpType
     calls = _calls(core, T, topo, route)
-    by_relay = calls[0][1][0][0] == "dram"
+    by_relay = len(_sets(core, T, topo, route)[2]) > 0
 
+    SY.dma_start(T.kd[:, :], T.keep[:, :]).then_inc(S.ldkd, 16)
     if by_relay:
         SC.dma_start(T.xd[:, :], T.x[:, :]).then_inc(S.ldd, 16)
-        SY.dma_start(T.kd[:, :], T.keep[:, :]).then_inc(S.ldkd, 16)
         SY.dma_start(T.F[:, rank:rank + 1], T.keep[:, :]).then_inc(S.ldk, 16)
         SY.dma_start(slot(rank), T.x[:, :]).then_inc(S.ldx, 16)
     else:
@@ -206,14 +210,19 @@ def rank_program(g, core, T, topo):
         sent += len(_bits(m))
     g.remote_dma_fused(tl, local_sem=S.snt)
 
-    i1 = done(g.iota(T.Ji[:, 128:129], [[0, 1]], 0, 1))
     ko32 = done(V.memset(T.o32[:, :], 1.0))
     zz = done(V.memset(T.win[:, 0:ZPAD], 0.0))
+    kown = [done(V.memset(entry(r), ZPAD + NCOL * r)) for r, s in enumerate(T.cores)
+            if topo.chip(s) != topo.chip(core) and route[(s, core)] is None]
     need(V, ko32)
     kjf = done(V.tensor_tensor_scan(T.Jf[:, :], T.o32[:, :], T.o32[:, :], -1.0, Op.mult, Op.add))
     need(V, kjf)
+    kjt = done(V.transpose(T.JT[:, :], T.Jf[:, :]))
     i0 = done(V.tensor_copy(T.Ji[:, 0:128], T.Jf[:, :]))
-    need(V, i0, i1)
+    need(V, kjt)
+    i1 = [done(V.tensor_copy(T.Ji[32 * a:32 * a + 32, 128:129], T.JT[32 * a:32 * a + 32, 32 * a:32 * a + 1]))
+          for a in range(4)]
+    need(V, i0, *i1)
     k1 = done(V.tensor_scalar(T.L7[:, :], T.Ji[:, :], 7, None, Op.bitwise_and))
     k2 = done(V.tensor_scalar(T.H3[:, :], T.Ji[:, :], 3, None, Op.logical_shift_right))
     k8 = done(V.tensor_scalar(T.I15[:, :], T.Ji[:, 0:128], 15, None, Op.bitwise_and))
@@ -231,6 +240,7 @@ def rank_program(g, core, T, topo):
     need(V, k5)
     ksl = done(V.tensor_scalar(T.SL[:, :], T.TQ[:, 0:128], T.tqf[:, 0:1], None, Op.is_gt))
     V.wait_ge(S.ti, 1)
+    need(V, *kown)
     V.wait_ge(S.tb, exp[(core, "tb")])
     kwc = [done(V.tensor_scalar(T.Wc[:, r:r + 1], entry(r), T.tqf[:, 0:1], None, Op.add)) for r in range(4)]
     need(V, kone, kc16, ki16, *kwc)
@@ -240,7 +250,7 @@ def rank_program(g, core, T, topo):
         if first[kind]:
             first[kind] = False
             if kind == "fl":
-                g.wait_ge(S.ldkd if by_relay else S.ldk, 16)
+                g.wait_ge(S.ldkd, 16)
             else:
                 g.wait_ge(S.ldd if by_relay else S.ldx, 16)
         tl = []

from concourse.bass import DstId, RemoteDMATransfer
from concourse.mybir import AluOpType, ActivationFunctionType

NCOL, OUTW, ZPAD = 128, 448, 4
WINW = ZPAD + 4 * NCOL
NSEM = 60

SCRATCH = {
    "win": ("sbuf", [128, WINW], "float32"),
    "yb": ("sbuf", [128, OUTW], "float32"),
    "F": ("sbuf", [128, 4], "int32"),
    "kd": ("dram", [128, 1], "int32"),
    "xd": ("dram", [128, NCOL], "float32"),
    "o32": ("sbuf", [128, 128], "float32"),
    "Jf": ("sbuf", [128, 128], "float32"),
    "JT": ("sbuf", [128, 128], "float32"),
    "Ji": ("sbuf", [128, 129], "int32"),
    "L7": ("sbuf", [128, 129], "int32"),
    "H3": ("sbuf", [128, 129], "int32"),
    "L16": ("sbuf", [128, 129], "int32"),
    "TQ": ("sbuf", [128, 129], "int32"),
    "I15": ("sbuf", [128, 128], "int32"),
    "tqf": ("sbuf", [128, 1], "float32"),
    "TB": ("sbuf", [128, 16], "int32"),
    "Wc": ("sbuf", [128, 4], "int32"),
    "WK": ("sbuf", [128, 4], "float32"),
    "SL": ("sbuf", [128, 128], "float16"),
    "one": ("sbuf", [128, 128], "float16"),
    "I16": ("sbuf", [128, 128], "float16"),
    "C16": ("sbuf", [128, 28], "float16"),
    "Ff": ("sbuf", [128, 4], "float16"),
    "G": ("sbuf", [128, 4], "float16"),
    "a16": ("sbuf", [128, 4], "float32"),
    "V": ("sbuf", [128, 4 * 128], "float16"),
    "A": ("sbuf", [128, 4 * 28], "float16"),
    "off": ("sbuf", [128, 28], "uint16"),
    "pE": ("psum", [128, 512], "float32"),
    "pO": ("psum", [128, 512], "float32"),
}
SEMAPHORES = ["ldk", "ldx", "ldkd", "ldd", "fl", "dat", "snt", "st", "tb", "ti"] + ["c%d" % k for k in range(NSEM)]


def _bits(m):
    return [b for b in range(16) if (m >> b) & 1]


def _mk(bits):
    m = 0
    for b in bits:
        m |= 1 << b
    return m


def _plan(T, topo):
    ranks = list(T.cores)
    used = set(ranks)
    route = {}
    for s in ranks:
        for d in ranks:
            if d == s:
                continue
            if topo.may_write(s, d):
                route[(s, d)] = None
                continue
            cand = [c for c in range(topo.CHIPS * topo.CORES_PER_CHIP)
                    if topo.chip(c) == topo.chip(s) and c not in used and topo.may_write(c, d)]
            cand.sort(key=lambda c: (topo.die(c) != topo.die(s), c))
            route[(s, d)] = cand[0]
            used.add(cand[0])
    return route


def _sets(s, T, topo, route):
    others = [d for d in T.cores if d != s]
    near = [d for d in others if topo.chip(d) == topo.chip(s)]
    far = [d for d in others if topo.chip(d) != topo.chip(s) and route[(s, d)] is None]
    rel = [route[(s, d)] for d in others if route[(s, d)] is not None]
    return near, far, rel


def _masks(s, T, topo, route):
    near, far, rel = _sets(s, T, topo, route)
    full = topo.mask(s, near[0])
    for c in near + rel:
        full &= topo.mask(s, c)
    moff = full
    for c in far:
        moff &= topo.mask(s, c)
    return moff, full & ~moff, full


def _early(s, T, topo, route):
    near, far, _rel = _sets(s, T, topo, route)
    moff, _mon, full = _masks(s, T, topo, route)
    if far:
        return [(near, moff)]
    b = _bits(full)
    return [(near, _mk(b[len(b) // 2:]))]


def _calls(s, T, topo, route):
    near, far, rel = _sets(s, T, topo, route)
    moff, mon, full = _masks(s, T, topo, route)
    calls = []
    if rel:
        b = _bits(full)
        one, hi = _mk(b[:1]), _mk(b[len(b) // 2:])
        calls.append(("fl", [("dram", [(c, "dram") for c in rel], one), ("dram", [(c, "sbuf") for c in near], hi)]))
        calls.append(("dat", [("dram", [(c, "dram") for c in rel], full)]))
        calls.append(("dat", [("dram", [(c, "sbuf") for c in near], full)]))
    else:
        b = _bits(mon)
        calls.append(("fl", [("dram", [(c, "sbuf") for c in far], moff),
                             ("dram", [(c, "sbuf") for c in near], _mk(b[:len(b) // 2]))]))
        calls.append(("dat", [("sbuf", [(c, "sbuf") for c in far], moff), ("sbuf", [(c, "sbuf") for c in near], mon)]))
    return calls


def _expected(T, topo, route):
    exp = {}

    def add(c, kind, m):
        exp[(c, kind)] = exp.get((c, kind), 0) + len(_bits(m))

    for s in T.cores:
        for dsts, m in _early(s, T, topo, route):
            for c in dsts:
                add(c, "tb", m)
        for kind, trs in _calls(s, T, topo, route):
            for _src, dsts, m in trs:
                for c, _w in dsts:
                    add(c, kind, m)
    for (_s, d), c in route.items():
        if c is not None:
            for kind in ("tb", "fl", "dat"):
                add(d, kind, topo.mask(c, d))
    return exp


def rank_program(g, core, T, topo):
    route = _plan(T, topo)
    exp = _expected(T, topo, route)
    S = T.sem
    V, PE, SC, SY = g.vector, g.tensor, g.scalar, g.sync

    def slot(r):
        return T.win[:, ZPAD + NCOL * r:ZPAD + NCOL * (r + 1)]

    def entry(r):
        return T.TB[:, 4 * r:4 * r + 1]

    for (s, d), c in route.items():
        if c == core:
            r = T.rank_of(s)
            rid, pid, _se = topo.addr(d)
            m = topo.mask(core, d)
            V.memset(entry(r), ZPAD + NCOL * r).then_inc(S.ti, 1)
            g.wait_ge(S.ti, 1)
            g.remote_dma(out_ap=entry(r), in_ap=entry(r), remote_sem=S.tb, local_sem=S.snt,
                         pid=pid, routing_id=rid, dma_engine_mask=m)
            g.wait_ge(S.fl, exp[(core, "fl")])
            g.remote_dma(out_ap=T.F[:, r:r + 1], in_ap=T.kd[:, :], remote_sem=S.fl, local_sem=S.snt,
                         pid=pid, routing_id=rid, dma_engine_mask=m)
            g.wait_ge(S.dat, exp[(core, "dat")])
            g.remote_dma(out_ap=slot(r), in_ap=T.xd[:, :], remote_sem=S.dat, local_sem=S.snt,
                         pid=pid, routing_id=rid, dma_engine_mask=m)
            g.wait_ge(S.snt, 3 * len(_bits(m)))
            return
    rank = T.rank_of(core)
    if rank is None:
        return

    Op = AluOpType
    calls = _calls(core, T, topo, route)
    by_relay = len(_sets(core, T, topo, route)[2]) > 0

    SY.dma_start(T.kd[:, :], T.keep[:, :]).then_inc(S.ldkd, 16)
    if by_relay:
        SC.dma_start(T.xd[:, :], T.x[:, :]).then_inc(S.ldd, 16)
        SY.dma_start(T.F[:, rank:rank + 1], T.keep[:, :]).then_inc(S.ldk, 16)
        SY.dma_start(slot(rank), T.x[:, :]).then_inc(S.ldx, 16)
    else:
        SC.dma_start(slot(rank), T.x[:, :]).then_inc(S.ldx, 16)
        SY.dma_start(T.F[:, rank:rank + 1], T.keep[:, :]).then_inc(S.ldk, 16)

    n = [0]
    seen = set()

    def done(inst):
        k = n[0]
        n[0] += 1
        inst.then_inc(S["c%d" % k], 1)
        return k

    def need(q, *ks):
        for k in ks:
            q.wait_ge(S["c%d" % k], 1)
            seen.add(k)

    def ids(cs):
        return [DstId(rid=topo.addr(c)[0], pnc=topo.addr(c)[1]) for c in cs]

    V.memset(entry(rank), ZPAD + NCOL * rank).then_inc(S.ti, 1)
    g.wait_ge(S.ti, 1)
    sent = 0
    tl = []
    for dsts, m in _early(core, T, topo, route):
        tl.append(RemoteDMATransfer(dst_ids=ids(dsts), dma_engine_mask=m, remote_sem=S.tb, srcs=[entry(rank)],
                                    dsts=[entry(rank) for _c in dsts]))
        sent += len(_bits(m))
    g.remote_dma_fused(tl, local_sem=S.snt)

    ko32 = done(V.memset(T.o32[:, :], 1.0))
    zz = done(V.memset(T.win[:, 0:ZPAD], 0.0))
    kown = [done(V.memset(entry(r), ZPAD + NCOL * r)) for r, s in enumerate(T.cores)
            if topo.chip(s) != topo.chip(core) and route[(s, core)] is None]
    need(V, ko32)
    kjf = done(V.tensor_tensor_scan(T.Jf[:, :], T.o32[:, :], T.o32[:, :], -1.0, Op.mult, Op.add))
    need(V, kjf)
    kjt = done(V.transpose(T.JT[:, :], T.Jf[:, :]))
    i0 = done(V.tensor_copy(T.Ji[:, 0:128], T.Jf[:, :]))
    need(V, kjt)
    i1 = [done(V.tensor_copy(T.Ji[32 * a:32 * a + 32, 128:129], T.JT[32 * a:32 * a + 32, 32 * a:32 * a + 1]))
          for a in range(4)]
    need(V, i0, *i1)
    k1 = done(V.tensor_scalar(T.L7[:, :], T.Ji[:, :], 7, None, Op.bitwise_and))
    k2 = done(V.tensor_scalar(T.H3[:, :], T.Ji[:, :], 3, None, Op.logical_shift_right))
    k8 = done(V.tensor_scalar(T.I15[:, :], T.Ji[:, 0:128], 15, None, Op.bitwise_and))
    kone = done(V.tensor_scalar(T.one[:, :], T.Ji[:, 0:128], 0.0, None, Op.is_ge))
    kc16 = done(V.tensor_scalar(T.C16[:, :], T.Ji[:, 0:28], 16.0, None, Op.mult))
    kg0 = done(V.tensor_scalar(T.G[:, 0:1], T.Ji[:, 0:1], 0.0, -0.05859375, Op.mult, Op.add))
    need(V, k1)
    k3 = done(V.tensor_scalar(T.L16[:, :], T.L7[:, :], 16.0, None, Op.mult))
    need(V, k8)
    ki16 = done(V.tensor_scalar(T.I16[:, :], T.I15[:, :], -7.5, None, Op.add))
    need(V, k2, k3)
    k4 = done(V.tensor_tensor(T.TQ[:, :], T.L16[:, :], T.H3[:, :], Op.add))
    need(V, k4)
    k5 = done(V.tensor_copy(T.tqf[:, :], T.TQ[:, 128:129]))
    need(V, k5)
    ksl = done(V.tensor_scalar(T.SL[:, :], T.TQ[:, 0:128], T.tqf[:, 0:1], None, Op.is_gt))
    V.wait_ge(S.ti, 1)
    need(V, *kown)
    V.wait_ge(S.tb, exp[(core, "tb")])
    kwc = [done(V.tensor_scalar(T.Wc[:, r:r + 1], entry(r), T.tqf[:, 0:1], None, Op.add)) for r in range(4)]
    need(V, kone, kc16, ki16, *kwc)

    first = {"fl": True, "dat": True}
    for kind, trs in calls:
        if first[kind]:
            first[kind] = False
            if kind == "fl":
                g.wait_ge(S.ldkd, 16)
            else:
                g.wait_ge(S.ldd if by_relay else S.ldx, 16)
        tl = []
        for src, dsts, m in trs:
            if kind == "fl":
                sap = T.kd[:, :] if src == "dram" else T.F[:, rank:rank + 1]
                daps = [T.kd[:, :] if w == "dram" else T.F[:, rank:rank + 1] for _c, w in dsts]
            else:
                sap = T.xd[:, :] if src == "dram" else slot(rank)
                daps = [T.xd[:, :] if w == "dram" else slot(rank) for _c, w in dsts]
            tl.append(RemoteDMATransfer(dst_ids=ids([c for c, _w in dsts]), dma_engine_mask=m, remote_sem=S[kind],
                                        srcs=[sap], dsts=daps))
            sent += len(_bits(m))
        g.remote_dma_fused(tl, local_sem=S.snt)

    V.wait_ge(S.ldk, 16)
    V.wait_ge(S.fl, exp[(core, "fl")])
    kf = done(V.tensor_copy(T.Ff[:, :], T.F[:, :]))
    need(V, kf)
    kg = done(V.tensor_tensor_scan(T.G[:, 1:4], T.one[:, 0:3], T.Ff[:, 0:3], -0.05859375, Op.mult, Op.add))
    kwk = done(V.tensor_tensor(T.WK[:, :], T.F[:, :], T.Wc[:, :], Op.mult))
    need(PE, ksl, kone, kf)
    PE.matmul(T.pE[:, 0:4], T.SL[:, :], T.Ff[:, :], True, False)
    need(PE, kg0, kg)
    ke = done(PE.matmul(T.pE[:, 0:4], T.one[:, :], T.G[:, :], False, True))
    need(V, ke)
    big = 201326592.0
    ka = done(V.tensor_scalar(T.a16[:, :], T.pE[:, 0:4], big, big, Op.add, Op.subtract))
    need(V, ka, kwk)
    ko = None
    for r in range(4):
        kv = done(V.tensor_scalar(T.V[:, 128 * r:128 * (r + 1)], T.I16[:, :], T.a16[:, r:r + 1], T.pE[:, r:r + 1],
                                  Op.add, Op.is_equal))
        kA = done(V.tensor_scalar(T.A[:, 28 * r:28 * (r + 1)], T.C16[:, :], T.a16[:, r:r + 1], T.WK[:, r:r + 1],
                                  Op.is_equal, Op.mult))
        need(PE, kv, kA)
        mm = PE.matmul(T.pO[:, 0:28], T.V[:, 128 * r:128 * (r + 1)], T.A[:, 28 * r:28 * (r + 1)], r == 0, r == 3)
        if r == 3:
            ko = done(mm)
    need(V, ko)
    kl = done(V.tensor_copy(T.off[:, :], T.pO[:, 0:28]))

    need(V, kl, zz)
    V.wait_ge(S.ldx, 16)
    V.wait_ge(S.dat, exp[(core, "dat")])
    g1 = done(V.tensor_copy(T.yb[:, 0:224], T.win[:, 0:WINW].indirect(T.off[:, 0:14])))
    need(SC, kl, zz)
    SC.wait_ge(S.ldx, 16)
    SC.wait_ge(S.dat, exp[(core, "dat")])
    g2 = done(SC.activation(T.yb[:, 224:448], T.win[:, 0:WINW].indirect(T.off[:, 14:28]), ActivationFunctionType.Copy))
    need(SY, g1, g2)
    SY.dma_start(T.y[:, :], T.yb[:, :]).then_inc(S.st, 16)
    SY.wait_ge(S.st, 16)

    g.wait_ge(S.snt, sent)
    for k in range(n[0]):
        if k not in seen:
            g.wait_ge(S["c%d" % k], 1)
